import numpy as np
import ml_dtypes


def mxq(x, axis, fmt="e4m3"):
    dtype, down = {"e4m3": (ml_dtypes.float8_e4m3fn, 7), "e5m2": (ml_dtypes.float8_e5m2, 14)}[fmt]
    v = np.moveaxis(np.asarray(x, np.float32).astype(ml_dtypes.bfloat16).astype(np.float64), axis, -1)
    blocks = v.reshape(v.shape[:-1] + (-1, 32))
    amax = np.abs(blocks).max(-1, keepdims=True)
    byte = np.maximum(np.where(amax > 0, np.frexp(amax)[1] - 1 + 127, 0) - down, 1)
    scale = np.exp2(byte - 127.0)
    codes = (blocks / scale).astype(np.float32).astype(dtype).astype(np.float64)
    return np.moveaxis((codes * scale).reshape(v.shape), -1, axis)


WIDE = False


def mx_kscale(k):
    if not WIDE:
        return np.ones(k)
    levels = np.array([10, -10, 5, -5, 0])
    if k % 512:
        return np.exp2(np.random.permutation(np.resize(levels, k // 32))).repeat(32)
    a = np.empty((k // 512, 16))
    for p in range(k // 512):
        a[p, :8] = np.random.permutation(np.resize(levels, 8))
        for g in range(8):
            far = levels[np.abs(levels - a[p, g]) >= 10]
            a[p, g + 8] = far[np.random.randint(len(far))]
    return np.exp2(a.ravel()).repeat(32)


def f64(x):
    return np.asarray(x).astype(np.float64)


def striped(idx):
    return np.tile(idx.reshape(-1, 16).T, (8, 1)).astype(np.uint16)


def unstriped(offs):
    return offs[:16].T.reshape(-1).astype(np.int64)


def striped8(idx):
    return np.concatenate([x.reshape(-1, 16).T for x in idx]).astype(np.uint16)


def runs(offs, k):
    lists = np.stack([offs[16 * r : 16 * r + 16].T.reshape(-1) for r in range(8)]).astype(np.int64)
    return lists[np.arange(k) % 512 // 64]


def pack_weight(w):
    k, n = w.shape
    w = f64(np.asarray(w, np.float32).astype(ml_dtypes.bfloat16)).reshape(k // 32, 32, n)
    amax = np.abs(w).max(1)
    byte = np.clip(np.where(amax > 0, np.frexp(amax)[1] - 1 + 127 - 7, 1), 1, 254)
    scaled = (w * np.exp2(127.0 - byte)[:, None, :]).reshape(k, n).astype(np.float32)
    words = np.ascontiguousarray(scaled.reshape(k // 512, 128, 4, n).transpose(0, 1, 3, 2)).astype(ml_dtypes.float8_e4m3fn).view(np.uint8)
    return words, np.ascontiguousarray(byte.astype(np.uint8).reshape(k // 512, 16, n))


def unpack_weight(words, scales):
    g, p, n, _ = words.shape
    vals = np.ascontiguousarray(words).view(ml_dtypes.float8_e4m3fn).astype(np.float64) * np.repeat(np.exp2(scales.astype(np.float64) - 127.0), 8, axis=1)[..., None]
    return vals.transpose(0, 1, 3, 2).reshape(g * 512, n)


K, T, S, N, H, U = 512, 2048, 512, 512, 512, 1024


def setup_inputs():
    n = np.random.standard_normal
    s = mx_kscale(K)[:, None]
    u = mx_kscale(H)
    packed_xT = pack_weight(n((K, T)) * s)
    return {
        "x_words": packed_xT[0],
        "x_scales": packed_xT[1],
        "w1": (n((K, H)) / np.sqrt(K) / s).astype(np.float32),
        "w2": (n((K, H)) / np.sqrt(K) / s).astype(np.float32),
        "gn": (np.random.uniform(0.5, 1.5, (H, 1)) * u[:, None]).astype(np.float32),
        "w3": (n((H, N)) / np.sqrt(H) / u[:, None]).astype(np.float32),
        "mem": n((N, U)).astype(np.float32),
        "offs": striped(np.random.permutation(T)[:S]),
        "two": striped(np.random.permutation(T)[:S]),
        "n1": striped8(np.stack([np.random.permutation(S) for _ in range(8)])),
        "n2": striped8(np.stack([np.random.permutation(S) for _ in range(8)])),
        "n3": striped8(np.stack([np.random.permutation(U)[:S] for _ in range(8)])),
    }


def reference(x_words, x_scales, w1, w2, gn, w3, mem, offs, two, n1, n2, n3):
    xq = unpack_weight(x_words, x_scales)[:, unstriped(offs)]
    y = mxq(f64(w1), 0, "e4m3").T @ xq
    x_two = unpack_weight(x_words, x_scales)[:, unstriped(two)]
    d = mxq(f64(w2), 0, "e4m3").T @ x_two
    z = f64(gn) * (0.75 * (y * (d[np.arange(H)[:, None], runs(n2, H)]) - ((y[np.arange(H)[:, None], runs(n1, H)]) * d)))
    h = mxq(f64(w3), 0, "e4m3").T @ mxq(z, 0, "e4m3")
    out = f64(mem).copy()
    out[np.arange(N)[:, None], runs(n3, N)] = h
    return out

@@ -1,0 +1,209 @@
+from contextlib import ExitStack
+
+import concourse.mybir as mybir
+from concourse.masks import make_identity
+
+K, T, S, N, H, U = 512, 2048, 512, 512, 512, 1024
+FLOPS = 3 * 2 * 512 * 512 * 512
+
+F32 = mybir.dt.float32
+BF16 = mybir.dt.bfloat16
+I32 = mybir.dt.int32
+U32 = mybir.dt.uint32
+U16 = mybir.dt.uint16
+U8 = mybir.dt.uint8
+FP8X4 = mybir.dt.float8_e4m3fn_x4
+COPY = mybir.ActivationFunctionType.Copy
+MULT = mybir.AluOpType.mult
+
+P = 128
+PACK = 4
+CHUNK = 256
+CHUNKS = S // CHUNK
+BLOCKS = CHUNK // P
+LIST_COLS = CHUNK // 16
+
+
+def tile_picked_twlcrossbpage_none_p_kernel(
+    tc, x_words, x_scales, w1, w2, gn, w3, mem, offs, two, n1, n2, n3, out
+):
+    nc = tc.nc
+    with ExitStack() as ctx:
+        lists = ctx.enter_context(tc.tile_pool(name="lists", bufs=1))
+        keep = ctx.enter_context(tc.tile_pool(name="keep", bufs=1))
+        psum = ctx.enter_context(tc.psum_pool(name="psum", bufs=1))
+
+        def load_list(name, src):
+            tile = lists.tile([P, S // 16], U16, name=name)
+            nc.sync.dma_start(tile[:], src)
+            return tile
+
+        table_scales = keep.tile([P, T], U8, name="table_scales", tag="big3", align_bytes=64)
+        nc.gpsimd.memset(table_scales[:].bitcast(I32), 0)
+        for q in range(4):
+            nc.gpsimd.dma_start(
+                table_scales[32 * q : 32 * q + 4, :].bitcast(I32), x_scales[0, 4 * q : 4 * q + 4, :].bitcast(I32)
+            )
+
+        table_words = keep.tile([P, T], U32, name="table_words", tag="big0", align_bytes=64)
+        nc.sync.dma_start(table_words[:].bitcast(I32), x_words[0].rearrange("p n r -> p (n r)").bitcast(I32))
+        offs_l = load_list("offs_l", offs)
+        two_l = load_list("two_l", two)
+
+        def load_weight(name, tag, w):
+            raw = keep.tile([P, PACK, 512], F32, name=name, tag=tag, align_bytes=64)
+            nc.sync.dma_start(raw[:], w.rearrange("(p j) c -> p j c", j=PACK))
+            return raw
+
+        w1_raw = load_weight("w1_raw", "big1", w1)
+        w2_raw = load_weight("w2_raw", "big2", w2)
+        n2_l = load_list("n2_l", n2)
+        n1_l = load_list("n1_l", n1)
+        n3_l = load_list("n3_l", n3)
+
+        ident = keep.tile([P, P], F32, name="ident", align_bytes=64)
+        make_identity(nc, ident[:])
+
+        gn_rows = keep.tile([P, P], F32, name="gn_rows", tag="big4", align_bytes=64)
+        nc.vector.memset(gn_rows[:], 0.0)
+        nc.scalar.dma_start(
+            gn_rows[0:PACK, :].rearrange("t (a q) -> t a q", q=4), gn.rearrange("(a t q) o -> t a (q o)", t=PACK, q=4)
+        )
+        gn_turned = psum.tile([P, 512], F32, name="gn_turned", tag="words")
+        nc.tensor.transpose(gn_turned[:, 0:P], gn_rows[:], ident[:])
+        gain = keep.tile([P, PACK], F32, name="gain", align_bytes=64)
+        nc.scalar.activation(gain[:], gn_turned[:, 0:PACK], COPY, scale=0.75)
+
+        xa_words = keep.tile([P, S], U32, name="xa_words", align_bytes=64)
+        xb_words = keep.tile([P, S], U32, name="xb_words", align_bytes=64)
+        nc.vector.tensor_copy(xa_words[:], table_words[:].indirect(offs_l[:]))
+        nc.vector.tensor_copy(xb_words[:], table_words[:].indirect(two_l[:]))
+        picked_scales = keep.tile([P, 2, S], U8, name="picked_scales", tag="big0", align_bytes=64)
+        xa_scales, xb_scales = picked_scales[:, 0, :], picked_scales[:, 1, :]
+
+        def group_quarter(name, raw, t, copy):
+            grouped = keep.tile([P, P, PACK], BF16, name=name, align_bytes=64)
+            copy(
+                grouped[:].rearrange("p (a q) j -> p a j q", q=4),
+                raw[:].rearrange("p j (a t q) -> p t a j q", t=PACK, q=4)[:, t],
+            )
+            return grouped
+
+        def quantize(name, grouped, width):
+            codes = keep.tile([P, width], U32, name=name + "_codes", align_bytes=64)
+            scales = keep.tile([P, width], U8, name=name + "_scales", align_bytes=64)
+            nc.vector.quantize_mx(out=codes[:].bitcast(FP8X4), scales=scales[:], in_=grouped)
+            return codes, scales
+
+        def product(name, bank, lhs_codes, lhs_scales, rhs_codes, rhs_scales, width):
+            acc = psum.tile([P, 512], F32, name=name, tag=f"acc{bank % 3}")
+            nc.tensor.matmul_mx(
+                out=acc[:, 0:width],
+                lhsT=lhs_codes.bitcast(FP8X4),
+                lhsT_scale=lhs_scales,
+                rhs=rhs_codes.bitcast(FP8X4),
+                rhs_scale=rhs_scales,
+                start=True,
+                stop=True,
+            )
+            return acc
+
+        def quantize_quarter(name, grouped):
+            return quantize(name, grouped[:].rearrange("p m j -> p (m j)"), P)
+
+        w1_grouped = [group_quarter(f"w1_g{t}", w1_raw, t, nc.scalar.copy) for t in range(PACK)]
+        nc.vector.tensor_copy(xa_scales, table_scales[:].indirect(offs_l[:]))
+        w1_q = [quantize_quarter("w1_0", w1_grouped[0])]
+        nc.vector.tensor_copy(xb_scales, table_scales[:].indirect(two_l[:]))
+        w2_q = []
+        for t in range(PACK):
+            w2_grouped = group_quarter(f"w2_g{t}", w2_raw, t, nc.vector.tensor_copy)
+            if t + 1 < PACK:
+                w1_q.append(quantize_quarter(f"w1_{t + 1}", w1_grouped[t + 1]))
+            w2_q.append(quantize_quarter(f"w2_{t}", w2_grouped))
+
+        w3_raw = load_weight("w3_raw", "big1", w3)
+        pages = []
+        for t in range(PACK):
+            page = keep.tile([P, U], F32, name=f"page{t}", tag=("big3", "big4", "big2", "big0")[t], align_bytes=64)
+            nc.sync.dma_start(page[:], mem.rearrange("(p t) w -> t p w", t=PACK)[t])
+            pages.append(page)
+
+        y, y_neg, d = [], [], []
+        for t in range(PACK):
+            y_acc = product(f"y_acc{t}", 2 * t, w1_q[t][0][:], w1_q[t][1][:], xa_words[:], xa_scales, S)
+            d_acc = product(f"d_acc{t}", 2 * t + 1, w2_q[t][0][:], w2_q[t][1][:], xb_words[:], xb_scales, S)
+            y.append(keep.tile([P, S], F32, name=f"y{t}"))
+            y_neg.append(keep.tile([P, S], F32, name=f"y_neg{t}"))
+            d.append(keep.tile([P, S], F32, name=f"d{t}"))
+            nc.scalar.copy(y[t][:], y_acc[:])
+            nc.scalar.activation(y_neg[t][:], y_acc[:], COPY, scale=-1.0)
+            nc.scalar.activation(d[t][:], d_acc[:], COPY, scale=gain[:, t : t + 1])
+
+        def w3_half(half, tag):
+            grouped = keep.tile([P, 2, P, PACK], BF16, name=f"w3_grouped{half}", tag=tag, align_bytes=64)
+            nc.scalar.copy(
+                grouped[:].rearrange("p t m j -> p m j t"),
+                w3_raw[:].rearrange("p j (m t) -> p m j t", t=PACK)[:, :, :, 2 * half : 2 * half + 2],
+            )
+            return quantize(f"w3_{half}", grouped[:].rearrange("p t m j -> p (t m j)"), 2 * P)
+
+        w3_q = [w3_half(0, "gain")]
+
+        def chunk_list(tile, c):
+            return tile[:, c * LIST_COLS : (c + 1) * LIST_COLS]
+
+        def make_z(c):
+            cols = slice(c * CHUNK, (c + 1) * CHUNK)
+            z_turned = [psum.tile([P, PACK, P], F32, name=f"z_turned{c}{b}", tag="turned", bufs=4) for b in range(BLOCKS)]
+            for t in range(PACK):
+                last = (c, t) == (CHUNKS - 1, PACK - 1)
+                terms = keep.tile(
+                    [P, 2, CHUNK], F32, name=f"terms{c}{t}", tag="z_grouped0" if last else f"terms{c}{t}", align_bytes=64
+                )
+                nc.vector.tensor_tensor(terms[:, 0, :], d[t][:].indirect(chunk_list(n2_l, c)), y[t][:, cols], MULT)
+                nc.vector.tensor_tensor(terms[:, 1, :], y_neg[t][:].indirect(chunk_list(n1_l, c)), d[t][:, cols], MULT)
+                for b in range(BLOCKS):
+                    for term in range(2):
+                        nc.tensor.matmul(
+                            z_turned[b][:, t, :],
+                            terms[:, term, b * P : (b + 1) * P],
+                            ident[:],
+                            start=term == 0,
+                            stop=term == 1,
+                            is_transpose=True,
+                        )
+            z_words = psum.tile([P, BLOCKS, 2, P], F32, name=f"z_words{c}", tag="words")
+            for b in range(BLOCKS):
+                z_pairs = keep.tile([P, 2, P, 2], BF16, name=f"z_pairs{c}{b}", align_bytes=64)
+                nc.scalar.copy(
+                    z_pairs[:].rearrange("s u (a t) e -> s u a t e", t=PACK),
+                    z_turned[b][:].rearrange("s t (a u e) -> s u a t e", u=2, e=2),
+                )
+                pairs = z_pairs[:].rearrange("s u p e -> s (u p e)").bitcast(F32)
+                for u in range(2):
+                    nc.tensor.transpose(z_words[:, b, u, :], pairs[:, u * P : (u + 1) * P], ident[:])
+            z_grouped = keep.tile([P, BLOCKS, P, 2], F32, name=f"z_grouped{c}", align_bytes=64)
+            nc.scalar.copy(z_grouped[:], z_words[:].rearrange("p b u s -> p b s u"))
+            return quantize(f"z{c}", z_grouped[:].rearrange("p b s u -> p (b s u)").bitcast(BF16), CHUNK)
+
+        def h_product(c, t, z_q):
+            rows = slice(t % 2 * P, (t % 2 + 1) * P)
+            codes, scales = w3_q[t // 2]
+            return product(f"h_acc{c}{t}", c * PACK + t, codes[:, rows], scales[:, rows], z_q[0][:], z_q[1][:], CHUNK)
+
+        def put(c, t, h_acc, tag):
+            h = keep.tile([P, CHUNK], F32, name=f"h{c}{t}", tag=tag, align_bytes=64)
+            nc.scalar.copy(h[:], h_acc[:, 0:CHUNK])
+            nc.vector.tensor_copy(pages[t][:].indirect(chunk_list(n3_l, c)), h[:])
+
+        z_first = make_z(0)
+        for t in range(2):
+            put(0, t, h_product(0, t, z_first), f"h0{t}")
+        w3_q.append(w3_half(1, "z_pairs01"))
+        z_second = make_z(1)
+        for t in range(2, PACK):
+            put(0, t, h_product(0, t, z_first), f"z_pairs1{t - 2}")
+        for t in range(PACK):
+            put(1, t, h_product(1, t, z_second), f"h1{t}")
+            nc.sync.dma_start(out.rearrange("(p t) w -> t p w", t=PACK)[t], pages[t][:])

@@ -41,7 +41,7 @@ def tile_picked_twlcrossbpage_none_p_kernel(
         table_scales = keep.tile([P, T], U8, name="table_scales", tag="big3", align_bytes=64)
         nc.gpsimd.memset(table_scales[:].bitcast(I32), 0)
         for q in range(4):
-            nc.gpsimd.dma_start(
+            nc.scalar.dma_start(
                 table_scales[32 * q : 32 * q + 4, :].bitcast(I32), x_scales[0, 4 * q : 4 * q + 4, :].bitcast(I32)
             )
 
@@ -66,7 +66,7 @@ def tile_picked_twlcrossbpage_none_p_kernel(
 
         gn_rows = keep.tile([P, P], F32, name="gn_rows", tag="big4", align_bytes=64)
         nc.vector.memset(gn_rows[:], 0.0)
-        nc.scalar.dma_start(
+        nc.gpsimd.dma_start(
             gn_rows[0:PACK, :].rearrange("t (a q) -> t a q", q=4), gn.rearrange("(a t q) o -> t a (q o)", t=PACK, q=4)
         )
         gn_turned = psum.tile([P, 512], F32, name="gn_turned", tag="words")

@@ -45,16 +45,20 @@ def tile_picked_twlcrossbpage_none_p_kernel(
                 table_scales[32 * q : 32 * q + 4, :].bitcast(I32), x_scales[0, 4 * q : 4 * q + 4, :].bitcast(I32)
             )
 
-        table_words = keep.tile([P, T], U32, name="table_words", tag="big0", align_bytes=64)
-        nc.sync.dma_start(table_words[:].bitcast(I32), x_words[0].rearrange("p n r -> p (n r)").bitcast(I32))
-        offs_l = load_list("offs_l", offs)
-        two_l = load_list("two_l", two)
-
         def load_weight(name, tag, w):
             raw = keep.tile([P, PACK, 512], F32, name=name, tag=tag, align_bytes=64)
             nc.sync.dma_start(raw[:], w.rearrange("(p j) c -> p j c", j=PACK))
             return raw
 
+        offs_l = load_list("offs_l", offs)
+        table_words = keep.tile([P, T], U32, name="table_words", tag="big0", align_bytes=64)
+        nc.sync.dma_start(table_words[:].bitcast(I32), x_words[0].rearrange("p n r -> p (n r)").bitcast(I32))
+        two_l = load_list("two_l", two)
+        gn_rows = keep.tile([P, P], F32, name="gn_rows", tag="big4", align_bytes=64)
+        nc.vector.memset(gn_rows[:], 0.0)
+        nc.sync.dma_start(
+            gn_rows[0:PACK, :].rearrange("t (a q) -> t a q", q=4), gn.rearrange("(a t q) o -> t a (q o)", t=PACK, q=4)
+        )
         w1_raw = load_weight("w1_raw", "big1", w1)
         w2_raw = load_weight("w2_raw", "big2", w2)
         n2_l = load_list("n2_l", n2)
@@ -64,30 +68,21 @@ def tile_picked_twlcrossbpage_none_p_kernel(
         ident = keep.tile([P, P], F32, name="ident", align_bytes=64)
         make_identity(nc, ident[:])
 
-        gn_rows = keep.tile([P, P], F32, name="gn_rows", tag="big4", align_bytes=64)
-        nc.vector.memset(gn_rows[:], 0.0)
-        nc.gpsimd.dma_start(
-            gn_rows[0:PACK, :].rearrange("t (a q) -> t a q", q=4), gn.rearrange("(a t q) o -> t a (q o)", t=PACK, q=4)
-        )
         gn_turned = psum.tile([P, 512], F32, name="gn_turned", tag="words")
         nc.tensor.transpose(gn_turned[:, 0:P], gn_rows[:], ident[:])
         gain = keep.tile([P, PACK], F32, name="gain", align_bytes=64)
         nc.scalar.activation(gain[:], gn_turned[:, 0:PACK], COPY, scale=0.75)
 
-        xa_words = keep.tile([P, S], U32, name="xa_words", align_bytes=64)
-        xb_words = keep.tile([P, S], U32, name="xb_words", align_bytes=64)
-        nc.vector.tensor_copy(xa_words[:], table_words[:].indirect(offs_l[:]))
-        nc.vector.tensor_copy(xb_words[:], table_words[:].indirect(two_l[:]))
-        picked_scales = keep.tile([P, 2, S], U8, name="picked_scales", tag="big0", align_bytes=64)
-        xa_scales, xb_scales = picked_scales[:, 0, :], picked_scales[:, 1, :]
+        def gather(picked, table, offsets):
+            nc.vector.tensor_copy(picked, table[:].indirect(offsets[:]))
 
-        def group_quarter(name, raw, t, copy):
-            grouped = keep.tile([P, P, PACK], BF16, name=name, align_bytes=64)
+        def group(name, raw, first, count, copy):
+            grouped = keep.tile([P, count, P, PACK], BF16, name=name, align_bytes=64)
             copy(
-                grouped[:].rearrange("p (a q) j -> p a j q", q=4),
-                raw[:].rearrange("p j (a t q) -> p t a j q", t=PACK, q=4)[:, t],
+                grouped[:].rearrange("p t (a q) j -> p t a j q", q=4),
+                raw[:].rearrange("p j (a t q) -> p t a j q", t=PACK, q=4)[:, first : first + count],
             )
-            return grouped
+            return grouped[:].rearrange("p t m j -> p (t m j)")
 
         def quantize(name, grouped, width):
             codes = keep.tile([P, width], U32, name=name + "_codes", align_bytes=64)
@@ -108,19 +103,33 @@ def tile_picked_twlcrossbpage_none_p_kernel(
             )
             return acc
 
-        def quantize_quarter(name, grouped):
-            return quantize(name, grouped[:].rearrange("p m j -> p (m j)"), P)
+        def columns(quantized, count):
+            codes, scales = quantized
+            return [(codes[:, i * P : (i + 1) * P], scales[:, i * P : (i + 1) * P]) for i in range(count)]
 
-        w1_grouped = [group_quarter(f"w1_g{t}", w1_raw, t, nc.scalar.copy) for t in range(PACK)]
-        nc.vector.tensor_copy(xa_scales, table_scales[:].indirect(offs_l[:]))
-        w1_q = [quantize_quarter("w1_0", w1_grouped[0])]
-        nc.vector.tensor_copy(xb_scales, table_scales[:].indirect(two_l[:]))
-        w2_q = []
-        for t in range(PACK):
-            w2_grouped = group_quarter(f"w2_g{t}", w2_raw, t, nc.vector.tensor_copy)
-            if t + 1 < PACK:
-                w1_q.append(quantize_quarter(f"w1_{t + 1}", w1_grouped[t + 1]))
-            w2_q.append(quantize_quarter(f"w2_{t}", w2_grouped))
+        xa_words = keep.tile([P, S], U32, name="xa_words", align_bytes=64)
+        xb_words = keep.tile([P, S], U32, name="xb_words", align_bytes=64)
+        gather(xa_words[:], table_words, offs_l)
+        gather(xb_words[:], table_words, two_l)
+        xa_scales = keep.tile([P, S], U8, name="xa_scales", tag="big0", align_bytes=64)[:]
+
+        parts = ((0, 1), (1, 1), (2, 2))
+        w1_grouped = [group(f"w1_grouped{t}", w1_raw, t, count, nc.scalar.copy) for t, count in parts]
+
+        def quantize_part(name, grouped, part):
+            count = parts[part][1]
+            return columns(quantize(f"{name}_{part}", grouped[part], count * P), count)
+
+        gather(xa_scales, table_scales, offs_l)
+        w1_q = quantize_part("w1", w1_grouped, 0)
+        xb_scales = keep.tile([P, S], U8, name="xb_scales", tag="w1_grouped0", align_bytes=64)[:]
+        gather(xb_scales, table_scales, two_l)
+        w2_grouped, w2_q = [], []
+        for part, (t, count) in enumerate(parts):
+            w2_grouped.append(group(f"w2_grouped{t}", w2_raw, t, count, nc.vector.tensor_copy))
+            if part + 1 < len(parts):
+                w1_q = w1_q + quantize_part("w1", w1_grouped, part + 1)
+            w2_q = w2_q + quantize_part("w2", w2_grouped, part)
 
         w3_raw = load_weight("w3_raw", "big1", w3)
         pages = []
@@ -131,13 +140,13 @@ def tile_picked_twlcrossbpage_none_p_kernel(
 
         y, y_neg, d = [], [], []
         for t in range(PACK):
-            y_acc = product(f"y_acc{t}", 2 * t, w1_q[t][0][:], w1_q[t][1][:], xa_words[:], xa_scales, S)
-            d_acc = product(f"d_acc{t}", 2 * t + 1, w2_q[t][0][:], w2_q[t][1][:], xb_words[:], xb_scales, S)
-            y.append(keep.tile([P, S], F32, name=f"y{t}"))
+            y_acc = product(f"y_acc{t}", 2 * t, w1_q[t][0], w1_q[t][1], xa_words[:], xa_scales, S)
+            d_acc = product(f"d_acc{t}", 2 * t + 1, w2_q[t][0], w2_q[t][1], xb_words[:], xb_scales, S)
+            y.append(keep.tile([P, CHUNK], F32, name=f"y{t}"))
             y_neg.append(keep.tile([P, S], F32, name=f"y_neg{t}"))
             d.append(keep.tile([P, S], F32, name=f"d{t}"))
-            nc.scalar.copy(y[t][:], y_acc[:])
             nc.scalar.activation(y_neg[t][:], y_acc[:], COPY, scale=-1.0)
+            nc.scalar.copy(y[t][:], y_acc[:, 0:CHUNK])
             nc.scalar.activation(d[t][:], d_acc[:], COPY, scale=gain[:, t : t + 1])
 
         def w3_half(half, tag):
@@ -148,25 +157,35 @@ def tile_picked_twlcrossbpage_none_p_kernel(
             )
             return quantize(f"w3_{half}", grouped[:].rearrange("p t m j -> p (t m j)"), 2 * P)
 
-        w3_q = [w3_half(0, "gain")]
+        late = keep.tile([P, PACK + 2 * (PACK - 1), CHUNK], F32, name="late", tag="gain", align_bytes=64)
+        y_late = late[:, 0:PACK, :]
+
+        def restore_y(t):
+            nc.scalar.activation(y_late[:, t, :], y_neg[t][:, CHUNK:S], COPY, scale=-1.0)
+
+        for t in range(PACK):
+            restore_y(t)
 
         def chunk_list(tile, c):
             return tile[:, c * LIST_COLS : (c + 1) * LIST_COLS]
 
         def make_z(c):
             cols = slice(c * CHUNK, (c + 1) * CHUNK)
-            z_turned = [psum.tile([P, PACK, P], F32, name=f"z_turned{c}{b}", tag="turned", bufs=4) for b in range(BLOCKS)]
+            z_turned = psum.tile([P, BLOCKS, PACK, P], F32, name=f"z_turned{c}", tag="turned")
             for t in range(PACK):
-                last = (c, t) == (CHUNKS - 1, PACK - 1)
-                terms = keep.tile(
-                    [P, 2, CHUNK], F32, name=f"terms{c}{t}", tag="z_grouped0" if last else f"terms{c}{t}", align_bytes=64
-                )
-                nc.vector.tensor_tensor(terms[:, 0, :], d[t][:].indirect(chunk_list(n2_l, c)), y[t][:, cols], MULT)
+                y_cols = y[t][:] if c == 0 else y_late[:, t, :]
+                if c == 0:
+                    terms = keep.tile([P, 2, CHUNK], F32, name=f"terms{t}", align_bytes=64)
+                elif t < PACK - 1:
+                    terms = late[:, PACK + 2 * t : PACK + 2 * t + 2, :]
+                else:
+                    terms = keep.tile([P, 2, CHUNK], F32, name="terms_last", tag="z_grouped0", align_bytes=64)
+                nc.vector.tensor_tensor(terms[:, 0, :], d[t][:].indirect(chunk_list(n2_l, c)), y_cols, MULT)
                 nc.vector.tensor_tensor(terms[:, 1, :], y_neg[t][:].indirect(chunk_list(n1_l, c)), d[t][:, cols], MULT)
                 for b in range(BLOCKS):
                     for term in range(2):
                         nc.tensor.matmul(
-                            z_turned[b][:, t, :],
+                            z_turned[:, b, t, :],
                             terms[:, term, b * P : (b + 1) * P],
                             ident[:],
                             start=term == 0,
@@ -178,7 +197,7 @@ def tile_picked_twlcrossbpage_none_p_kernel(
                 z_pairs = keep.tile([P, 2, P, 2], BF16, name=f"z_pairs{c}{b}", align_bytes=64)
                 nc.scalar.copy(
                     z_pairs[:].rearrange("s u (a t) e -> s u a t e", t=PACK),
-                    z_turned[b][:].rearrange("s t (a u e) -> s u a t e", u=2, e=2),
+                    z_turned[:, b].rearrange("s t (a u e) -> s u a t e", u=2, e=2),
                 )
                 pairs = z_pairs[:].rearrange("s u p e -> s (u p e)").bitcast(F32)
                 for u in range(2):
@@ -198,9 +217,10 @@ def tile_picked_twlcrossbpage_none_p_kernel(
             nc.vector.tensor_copy(pages[t][:].indirect(chunk_list(n3_l, c)), h[:])
 
         z_first = make_z(0)
+        w3_q = [w3_half(0, "z_pairs00")]
         for t in range(2):
             put(0, t, h_product(0, t, z_first), f"h0{t}")
-        w3_q.append(w3_half(1, "z_pairs01"))
+        w3_q.append(w3_half(1, "z_pairs00"))
         z_second = make_z(1)
         for t in range(2, PACK):
             put(0, t, h_product(0, t, z_first), f"z_pairs1{t - 2}")

@@ -91,7 +91,7 @@ def tile_picked_twlcrossbpage_none_p_kernel(
             return codes, scales
 
         def product(name, bank, lhs_codes, lhs_scales, rhs_codes, rhs_scales, width):
-            acc = psum.tile([P, 512], F32, name=name, tag=f"acc{bank % 3}")
+            acc = psum.tile([P, 512], F32, name=name, tag=bank)
             nc.tensor.matmul_mx(
                 out=acc[:, 0:width],
                 lhsT=lhs_codes.bitcast(FP8X4),
@@ -140,8 +140,8 @@ def tile_picked_twlcrossbpage_none_p_kernel(
 
         y, y_neg, d = [], [], []
         for t in range(PACK):
-            y_acc = product(f"y_acc{t}", 2 * t, w1_q[t][0], w1_q[t][1], xa_words[:], xa_scales, S)
-            d_acc = product(f"d_acc{t}", 2 * t + 1, w2_q[t][0], w2_q[t][1], xb_words[:], xb_scales, S)
+            y_acc = product(f"y_acc{t}", ("acc0", "acc2", "acc1", "acc2")[t], w1_q[t][0], w1_q[t][1], xa_words[:], xa_scales, S)
+            d_acc = product(f"d_acc{t}", ("acc1", "acc0", "turned", "acc0")[t], w2_q[t][0], w2_q[t][1], xb_words[:], xb_scales, S)
             y.append(keep.tile([P, CHUNK], F32, name=f"y{t}"))
             y_neg.append(keep.tile([P, S], F32, name=f"y_neg{t}"))
             d.append(keep.tile([P, S], F32, name=f"d{t}"))
@@ -157,14 +157,14 @@ def tile_picked_twlcrossbpage_none_p_kernel(
             )
             return quantize(f"w3_{half}", grouped[:].rearrange("p t m j -> p (t m j)"), 2 * P)
 
-        late = keep.tile([P, PACK + 2 * (PACK - 1), CHUNK], F32, name="late", tag="gain", align_bytes=64)
-        y_late = late[:, 0:PACK, :]
+        late = keep.tile([P, 1 + 2 * (PACK - 1), CHUNK], F32, name="late", tag="gain", align_bytes=64)
 
-        def restore_y(t):
-            nc.scalar.activation(y_late[:, t, :], y_neg[t][:, CHUNK:S], COPY, scale=-1.0)
+        def restore_y(t, target):
+            nc.scalar.activation(target, y_neg[t][:, CHUNK:S], COPY, scale=-1.0)
+            return target
 
-        for t in range(PACK):
-            restore_y(t)
+        y_late = [restore_y(0, late[:, 0, :])]
+        w3_q = [w3_half(0, "xb_words")]
 
         def chunk_list(tile, c):
             return tile[:, c * LIST_COLS : (c + 1) * LIST_COLS]
@@ -173,11 +173,11 @@ def tile_picked_twlcrossbpage_none_p_kernel(
             cols = slice(c * CHUNK, (c + 1) * CHUNK)
             z_turned = psum.tile([P, BLOCKS, PACK, P], F32, name=f"z_turned{c}", tag="turned")
             for t in range(PACK):
-                y_cols = y[t][:] if c == 0 else y_late[:, t, :]
+                y_cols = y[t][:] if c == 0 else y_late[t]
                 if c == 0:
                     terms = keep.tile([P, 2, CHUNK], F32, name=f"terms{t}", align_bytes=64)
                 elif t < PACK - 1:
-                    terms = late[:, PACK + 2 * t : PACK + 2 * t + 2, :]
+                    terms = late[:, 1 + 2 * t : 3 + 2 * t, :]
                 else:
                     terms = keep.tile([P, 2, CHUNK], F32, name="terms_last", tag="z_grouped0", align_bytes=64)
                 nc.vector.tensor_tensor(terms[:, 0, :], d[t][:].indirect(chunk_list(n2_l, c)), y_cols, MULT)
@@ -209,7 +209,7 @@ def tile_picked_twlcrossbpage_none_p_kernel(
         def h_product(c, t, z_q):
             rows = slice(t % 2 * P, (t % 2 + 1) * P)
             codes, scales = w3_q[t // 2]
-            return product(f"h_acc{c}{t}", c * PACK + t, codes[:, rows], scales[:, rows], z_q[0][:], z_q[1][:], CHUNK)
+            return product(f"h_acc{c}{t}", f"acc{(c * PACK + t) % 3}", codes[:, rows], scales[:, rows], z_q[0][:], z_q[1][:], CHUNK)
 
         def put(c, t, h_acc, tag):
             h = keep.tile([P, CHUNK], F32, name=f"h{c}{t}", tag=tag, align_bytes=64)
@@ -217,10 +217,11 @@ def tile_picked_twlcrossbpage_none_p_kernel(
             nc.vector.tensor_copy(pages[t][:].indirect(chunk_list(n3_l, c)), h[:])
 
         z_first = make_z(0)
-        w3_q = [w3_half(0, "z_pairs00")]
+        y_rest = keep.tile([P, PACK - 1, CHUNK], F32, name="y_rest", tag="z_pairs00", align_bytes=64)
+        y_late.extend([restore_y(t, y_rest[:, t - 1, :]) for t in range(1, PACK)])
         for t in range(2):
             put(0, t, h_product(0, t, z_first), f"h0{t}")
-        w3_q.append(w3_half(1, "z_pairs00"))
+        w3_q.append(w3_half(1, "z_pairs01"))
         z_second = make_z(1)
         for t in range(2, PACK):
             put(0, t, h_product(0, t, z_first), f"z_pairs1{t - 2}")

from contextlib import ExitStack

import concourse.mybir as mybir
from concourse.masks import make_identity

K, T, S, N, H, U = 512, 2048, 512, 512, 512, 1024
FLOPS = 3 * 2 * 512 * 512 * 512

F32 = mybir.dt.float32
BF16 = mybir.dt.bfloat16
I32 = mybir.dt.int32
U32 = mybir.dt.uint32
U16 = mybir.dt.uint16
U8 = mybir.dt.uint8
FP8X4 = mybir.dt.float8_e4m3fn_x4
COPY = mybir.ActivationFunctionType.Copy
MULT = mybir.AluOpType.mult

P = 128
PACK = 4
CHUNK = 256
CHUNKS = S // CHUNK
BLOCKS = CHUNK // P
LIST_COLS = CHUNK // 16


def tile_picked_twlcrossbpage_none_p_kernel(
    tc, x_words, x_scales, w1, w2, gn, w3, mem, offs, two, n1, n2, n3, out
):
    nc = tc.nc
    with ExitStack() as ctx:
        lists = ctx.enter_context(tc.tile_pool(name="lists", bufs=1))
        keep = ctx.enter_context(tc.tile_pool(name="keep", bufs=1))
        psum = ctx.enter_context(tc.psum_pool(name="psum", bufs=1))

        def load_list(name, src):
            tile = lists.tile([P, S // 16], U16, name=name)
            nc.sync.dma_start(tile[:], src)
            return tile

        table_scales = keep.tile([P, T], U8, name="table_scales", tag="big3", align_bytes=64)
        nc.gpsimd.memset(table_scales[:].bitcast(I32), 0)
        for q in range(4):
            nc.scalar.dma_start(
                table_scales[32 * q : 32 * q + 4, :].bitcast(I32), x_scales[0, 4 * q : 4 * q + 4, :].bitcast(I32)
            )

        def load_weight(name, tag, w):
            raw = keep.tile([P, PACK, 512], F32, name=name, tag=tag, align_bytes=64)
            nc.sync.dma_start(raw[:], w.rearrange("(p j) c -> p j c", j=PACK))
            return raw

        offs_l = load_list("offs_l", offs)
        table_words = keep.tile([P, T], U32, name="table_words", tag="big0", align_bytes=64)
        nc.sync.dma_start(table_words[:].bitcast(I32), x_words[0].rearrange("p n r -> p (n r)").bitcast(I32))
        two_l = load_list("two_l", two)
        gn_rows = keep.tile([P, P], F32, name="gn_rows", tag="big4", align_bytes=64)
        nc.vector.memset(gn_rows[:], 0.0)
        nc.sync.dma_start(
            gn_rows[0:PACK, :].rearrange("t (a q) -> t a q", q=4), gn.rearrange("(a t q) o -> t a (q o)", t=PACK, q=4)
        )
        w1_raw = load_weight("w1_raw", "big1", w1)
        w2_raw = load_weight("w2_raw", "big2", w2)
        n2_l = load_list("n2_l", n2)
        n1_l = load_list("n1_l", n1)
        n3_l = load_list("n3_l", n3)

        ident = keep.tile([P, P], F32, name="ident", align_bytes=64)
        make_identity(nc, ident[:])

        gn_turned = psum.tile([P, 512], F32, name="gn_turned", tag="words")
        nc.tensor.transpose(gn_turned[:, 0:P], gn_rows[:], ident[:])
        gain = keep.tile([P, PACK], F32, name="gain", align_bytes=64)
        nc.scalar.activation(gain[:], gn_turned[:, 0:PACK], COPY, scale=0.75)

        def gather(picked, table, offsets):
            nc.vector.tensor_copy(picked, table[:].indirect(offsets[:]))

        def group(name, raw, first, count, copy):
            grouped = keep.tile([P, count, P, PACK], BF16, name=name, align_bytes=64)
            copy(
                grouped[:].rearrange("p t (a q) j -> p t a j q", q=4),
                raw[:].rearrange("p j (a t q) -> p t a j q", t=PACK, q=4)[:, first : first + count],
            )
            return grouped[:].rearrange("p t m j -> p (t m j)")

        def quantize(name, grouped, width):
            codes = keep.tile([P, width], U32, name=name + "_codes", align_bytes=64)
            scales = keep.tile([P, width], U8, name=name + "_scales", align_bytes=64)
            nc.vector.quantize_mx(out=codes[:].bitcast(FP8X4), scales=scales[:], in_=grouped)
            return codes, scales

        def product(name, bank, lhs_codes, lhs_scales, rhs_codes, rhs_scales, width):
            acc = psum.tile([P, 512], F32, name=name, tag=bank)
            nc.tensor.matmul_mx(
                out=acc[:, 0:width],
                lhsT=lhs_codes.bitcast(FP8X4),
                lhsT_scale=lhs_scales,
                rhs=rhs_codes.bitcast(FP8X4),
                rhs_scale=rhs_scales,
                start=True,
                stop=True,
            )
            return acc

        def columns(quantized, count):
            codes, scales = quantized
            return [(codes[:, i * P : (i + 1) * P], scales[:, i * P : (i + 1) * P]) for i in range(count)]

        xa_words = keep.tile([P, S], U32, name="xa_words", align_bytes=64)
        xb_words = keep.tile([P, S], U32, name="xb_words", align_bytes=64)
        gather(xa_words[:], table_words, offs_l)
        gather(xb_words[:], table_words, two_l)
        xa_scales = keep.tile([P, S], U8, name="xa_scales", tag="big0", align_bytes=64)[:]

        parts = ((0, 1), (1, 1), (2, 2))
        w1_grouped = [group(f"w1_grouped{t}", w1_raw, t, count, nc.scalar.copy) for t, count in parts]

        def quantize_part(name, grouped, part):
            count = parts[part][1]
            return columns(quantize(f"{name}_{part}", grouped[part], count * P), count)

        gather(xa_scales, table_scales, offs_l)
        w1_q = quantize_part("w1", w1_grouped, 0)
        xb_scales = keep.tile([P, S], U8, name="xb_scales", tag="w1_grouped0", align_bytes=64)[:]
        gather(xb_scales, table_scales, two_l)
        w2_grouped, w2_q = [], []
        for part, (t, count) in enumerate(parts):
            w2_grouped.append(group(f"w2_grouped{t}", w2_raw, t, count, nc.vector.tensor_copy))
            if part + 1 < len(parts):
                w1_q = w1_q + quantize_part("w1", w1_grouped, part + 1)
            w2_q = w2_q + quantize_part("w2", w2_grouped, part)

        w3_raw = load_weight("w3_raw", "big1", w3)
        pages = []
        for t in range(PACK):
            page = keep.tile([P, U], F32, name=f"page{t}", tag=("big3", "big4", "big2", "big0")[t], align_bytes=64)
            nc.sync.dma_start(page[:], mem.rearrange("(p t) w -> t p w", t=PACK)[t])
            pages.append(page)

        y, y_neg, d = [], [], []
        for t in range(PACK):
            y_acc = product(f"y_acc{t}", ("acc0", "acc2", "acc1", "acc2")[t], w1_q[t][0], w1_q[t][1], xa_words[:], xa_scales, S)
            d_acc = product(f"d_acc{t}", ("acc1", "acc0", "turned", "acc0")[t], w2_q[t][0], w2_q[t][1], xb_words[:], xb_scales, S)
            y.append(keep.tile([P, CHUNK], F32, name=f"y{t}"))
            y_neg.append(keep.tile([P, S], F32, name=f"y_neg{t}"))
            d.append(keep.tile([P, S], F32, name=f"d{t}"))
            nc.scalar.activation(y_neg[t][:], y_acc[:], COPY, scale=-1.0)
            nc.scalar.copy(y[t][:], y_acc[:, 0:CHUNK])
            nc.scalar.activation(d[t][:], d_acc[:], COPY, scale=gain[:, t : t + 1])

        def w3_half(half, tag):
            grouped = keep.tile([P, 2, P, PACK], BF16, name=f"w3_grouped{half}", tag=tag, align_bytes=64)
            nc.scalar.copy(
                grouped[:].rearrange("p t m j -> p m j t"),
                w3_raw[:].rearrange("p j (m t) -> p m j t", t=PACK)[:, :, :, 2 * half : 2 * half + 2],
            )
            return quantize(f"w3_{half}", grouped[:].rearrange("p t m j -> p (t m j)"), 2 * P)

        late = keep.tile([P, 1 + 2 * (PACK - 1), CHUNK], F32, name="late", tag="gain", align_bytes=64)

        def restore_y(t, target):
            nc.scalar.activation(target, y_neg[t][:, CHUNK:S], COPY, scale=-1.0)
            return target

        y_late = [restore_y(0, late[:, 0, :])]
        w3_q = [w3_half(0, "xb_words")]

        def chunk_list(tile, c):
            return tile[:, c * LIST_COLS : (c + 1) * LIST_COLS]

        def make_z(c):
            cols = slice(c * CHUNK, (c + 1) * CHUNK)
            z_turned = psum.tile([P, BLOCKS, PACK, P], F32, name=f"z_turned{c}", tag="turned")
            for t in range(PACK):
                y_cols = y[t][:] if c == 0 else y_late[t]
                if c == 0:
                    terms = keep.tile([P, 2, CHUNK], F32, name=f"terms{t}", align_bytes=64)
                elif t < PACK - 1:
                    terms = late[:, 1 + 2 * t : 3 + 2 * t, :]
                else:
                    terms = keep.tile([P, 2, CHUNK], F32, name="terms_last", tag="z_grouped0", align_bytes=64)
                nc.vector.tensor_tensor(terms[:, 0, :], d[t][:].indirect(chunk_list(n2_l, c)), y_cols, MULT)
                nc.vector.tensor_tensor(terms[:, 1, :], y_neg[t][:].indirect(chunk_list(n1_l, c)), d[t][:, cols], MULT)
                for b in range(BLOCKS):
                    for term in range(2):
                        nc.tensor.matmul(
                            z_turned[:, b, t, :],
                            terms[:, term, b * P : (b + 1) * P],
                            ident[:],
                            start=term == 0,
                            stop=term == 1,
                            is_transpose=True,
                        )
            z_words = psum.tile([P, BLOCKS, 2, P], F32, name=f"z_words{c}", tag="words")
            for b in range(BLOCKS):
                z_pairs = keep.tile([P, 2, P, 2], BF16, name=f"z_pairs{c}{b}", align_bytes=64)
                nc.scalar.copy(
                    z_pairs[:].rearrange("s u (a t) e -> s u a t e", t=PACK),
                    z_turned[:, b].rearrange("s t (a u e) -> s u a t e", u=2, e=2),
                )
                pairs = z_pairs[:].rearrange("s u p e -> s (u p e)").bitcast(F32)
                for u in range(2):
                    nc.tensor.transpose(z_words[:, b, u, :], pairs[:, u * P : (u + 1) * P], ident[:])
            z_grouped = keep.tile([P, BLOCKS, P, 2], F32, name=f"z_grouped{c}", align_bytes=64)
            nc.scalar.copy(z_grouped[:], z_words[:].rearrange("p b u s -> p b s u"))
            return quantize(f"z{c}", z_grouped[:].rearrange("p b s u -> p (b s u)").bitcast(BF16), CHUNK)

        def h_product(c, t, z_q):
            rows = slice(t % 2 * P, (t % 2 + 1) * P)
            codes, scales = w3_q[t // 2]
            return product(f"h_acc{c}{t}", f"acc{(c * PACK + t) % 3}", codes[:, rows], scales[:, rows], z_q[0][:], z_q[1][:], CHUNK)

        def put(c, t, h_acc, tag):
            h = keep.tile([P, CHUNK], F32, name=f"h{c}{t}", tag=tag, align_bytes=64)
            nc.scalar.copy(h[:], h_acc[:, 0:CHUNK])
            nc.vector.tensor_copy(pages[t][:].indirect(chunk_list(n3_l, c)), h[:])

        z_first = make_z(0)
        y_rest = keep.tile([P, PACK - 1, CHUNK], F32, name="y_rest", tag="z_pairs00", align_bytes=64)
        y_late.extend([restore_y(t, y_rest[:, t - 1, :]) for t in range(1, PACK)])
        for t in range(2):
            put(0, t, h_product(0, t, z_first), f"h0{t}")
        w3_q.append(w3_half(1, "z_pairs01"))
        z_second = make_z(1)
        for t in range(2, PACK):
            put(0, t, h_product(0, t, z_first), f"z_pairs1{t - 2}")
        for t in range(PACK):
            put(1, t, h_product(1, t, z_second), f"h1{t}")
            nc.sync.dma_start(out.rearrange("(p t) w -> t p w", t=PACK)[t], pages[t][:])
